import numpy as np
import ml_dtypes


def mxq(x, axis, fmt="e4m3"):
    dtype, down = {"e4m3": (ml_dtypes.float8_e4m3fn, 7), "e5m2": (ml_dtypes.float8_e5m2, 14)}[fmt]
    v = np.moveaxis(np.asarray(x, np.float32).astype(ml_dtypes.bfloat16).astype(np.float64), axis, -1)
    blocks = v.reshape(v.shape[:-1] + (-1, 32))
    amax = np.abs(blocks).max(-1, keepdims=True)
    byte = np.maximum(np.where(amax > 0, np.frexp(amax)[1] - 1 + 127, 0) - down, 1)
    scale = np.exp2(byte - 127.0)
    codes = (blocks / scale).astype(np.float32).astype(dtype).astype(np.float64)
    return np.moveaxis((codes * scale).reshape(v.shape), -1, axis)


WIDE = False


def mx_kscale(k):
    if not WIDE:
        return np.ones(k)
    levels = np.array([10, -10, 5, -5, 0])
    if k % 512:
        return np.exp2(np.random.permutation(np.resize(levels, k // 32))).repeat(32)
    a = np.empty((k // 512, 16))
    for p in range(k // 512):
        a[p, :8] = np.random.permutation(np.resize(levels, 8))
        for g in range(8):
            far = levels[np.abs(levels - a[p, g]) >= 10]
            a[p, g + 8] = far[np.random.randint(len(far))]
    return np.exp2(a.ravel()).repeat(32)


def f64(x):
    return np.asarray(x).astype(np.float64)


E2M1 = np.array([0.0, 0.5, 1.0, 1.5, 2.0, 3.0, 4.0, 6.0, -0.0, -0.5, -1.0, -1.5, -2.0, -3.0, -4.0, -6.0])


def pack_weight(w, fmt):
    k, n = w.shape
    w = f64(np.asarray(w, np.float32).astype(ml_dtypes.bfloat16)).reshape(k // 32, 32, n)
    amax = np.abs(w).max(1)
    if fmt == "e4m3":
        byte = np.frexp(amax)[1] - 1 + 127 - 7
    else:
        mant, ex = np.frexp(amax / 6.0)
        byte = np.where(mant > 0.5, ex, ex - 1) + 127
    byte = np.clip(np.where(amax > 0, byte, 1), 1, 254)
    scaled = (w * np.exp2(127.0 - byte)[:, None, :]).reshape(k, n).astype(np.float32)
    by_word = np.ascontiguousarray(scaled.reshape(k // 512, 128, 4, n).transpose(0, 1, 3, 2))
    if fmt == "e4m3":
        words = by_word.astype(ml_dtypes.float8_e4m3fn).view(np.uint8)
    else:
        c = by_word.astype(ml_dtypes.float4_e2m1fn).view(np.uint8) & 0xF
        words = (c[..., 0::2] | (c[..., 1::2] << 4)).reshape(k // 512, 128, 2 * n)
    return np.ascontiguousarray(words), np.ascontiguousarray(byte.astype(np.uint8).reshape(k // 512, 16, n))


def unpack_weight(words, scales, fmt):
    g, _, n = scales.shape
    words = np.ascontiguousarray(words).reshape(g, 128, n, -1)
    if fmt == "e4m3":
        vals = words.view(ml_dtypes.float8_e4m3fn).astype(np.float64)
    else:
        nib = np.empty((g, 128, n, 4), np.uint8)
        nib[..., 0::2] = words & 0xF
        nib[..., 1::2] = words >> 4
        vals = E2M1[nib]
    vals = vals * np.repeat(np.exp2(scales.astype(np.float64) - 127.0), 8, axis=1)[..., None]
    return vals.transpose(0, 1, 3, 2).reshape(g * 512, n)


K, L, T, N = 1024, 1024, 512, 512


def setup_inputs():
    n = np.random.standard_normal
    fk = mx_kscale(K)
    fl = mx_kscale(L)
    xap = pack_weight(n((K, T)) / fk[:, None], "e4m3")
    xqp = pack_weight(n((L, T)) / fl[:, None], "e2m1")
    wqp = pack_weight(n((L, N)) * 1 / np.sqrt(L) * fl[:, None], "e4m3")
    wcp = pack_weight(n((K, N)) * 1 / np.sqrt(K) * fk[:, None], "e2m1")
    return {
        "xa_words": xap[0],
        "xa_scales": xap[1],
        "wa": (n((K, N)) * 1 / np.sqrt(K) * fk[:, None]).astype(np.float32),
        "xq_words": xqp[0],
        "xq_scales": xqp[1],
        "wq_words": wqp[0],
        "wq_scales": wqp[1],
        "wc_words": wcp[0],
        "wc_scales": wcp[1],
    }


def reference(xa_words, xa_scales, wa, xq_words, xq_scales, wq_words, wq_scales, wc_words, wc_scales):
    xau = unpack_weight(xa_words, xa_scales, "e4m3")
    xqu = unpack_weight(xq_words, xq_scales, "e2m1")
    wqu = unpack_weight(wq_words, wq_scales, "e4m3")
    wcu = unpack_weight(wc_words, wc_scales, "e2m1")
    waq = mxq(f64(wa), 0, "e4m3")
    p = waq.T @ xau + wqu.T @ xqu
    r = wcu.T @ xau
    y = np.maximum(p, 1.4 * r) - 0.25 * (p + r)
    return y

@@ -1,0 +1,215 @@
+from contextlib import ExitStack
+
+import concourse.mybir as mybir
+
+K, L, T, N = 1024, 1024, 512, 512
+FLOPS = 2 * N * T * (K + L + K)
+
+F32 = mybir.dt.float32
+BF16 = mybir.dt.bfloat16
+I32 = mybir.dt.int32
+U32 = mybir.dt.uint32
+U8 = mybir.dt.uint8
+FP8X4 = mybir.dt.float8_e4m3fn_x4
+FP4X4 = mybir.dt.float4_e2m1fn_x4
+ALU = mybir.AluOpType
+ACT = mybir.ActivationFunctionType
+
+P = 128
+PACK = 4
+PASSES = 2
+TILES = N // P
+HALF = T // 2
+
+
+def tile_mix_larger_of_two_sums_kernel(
+    tc, xa_words, xa_scales, wa, xq_words, xq_scales, wq_words, wq_scales, wc_words, wc_scales, out
+):
+    nc = tc.nc
+    with ExitStack() as ctx:
+        sb = ctx.enter_context(tc.tile_pool(name="sb", bufs=1))
+        ps = ctx.enter_context(tc.psum_pool(name="ps", bufs=1))
+        ctx.enter_context(tc.manual_schedule())
+
+        def new_plane(name):
+            plane = sb.tile([P, PASSES, 512], U8, name=name, align_bytes=64)
+            nc.vector.memset(plane[:].bitcast(I32), 0)
+            return plane
+
+        def load_plane(queue, plane, scales, quads):
+            for q in quads:
+                queue.dma_start(
+                    out=plane[32 * q : 32 * q + 4, :, :].bitcast(I32),
+                    in_=scales[:, 4 * q : 4 * q + 4, :].rearrange("z r c -> r z c").bitcast(I32),
+                )
+
+        def load_words(name, rows):
+            words = sb.tile([P, PASSES, rows.shape[2]], U8, name=name, align_bytes=64)
+            nc.sync.dma_start(out=words[:].bitcast(I32), in_=rows.bitcast(I32))
+            return words
+
+        xa_rows = xa_words.rearrange("z p c r -> p z (c r)")
+        wq_rows = wq_words.rearrange("z p c r -> p z (c r)")
+        xq_rows = xq_words.rearrange("z p c -> p z c")
+        wc_rows = wc_words.rearrange("z p c -> p z c")
+        wa_rows = wa.rearrange("(z p j) n -> z p j n", z=PASSES, j=PACK)
+
+        wa_raw, wa_bf, wa_codes, wa_plane = {}, {}, {}, {}
+
+        def load_wa_pass(i, z):
+            raw = sb.tile([P, PACK, P], F32, name="wa_raw_%d_%d" % (i, z))
+            nc.sync.dma_start(out=raw[:], in_=wa_rows[z, :, :, P * i : P * (i + 1)])
+            wa_raw[i, z] = raw
+
+        def load_wa(i):
+            for z in range(PASSES):
+                load_wa_pass(i, z)
+
+        def cast_wa(i, z, on_vector):
+            bf = sb.tile([P, P, PACK], BF16, name="wa_bf_%d_%d" % (i, z), align_bytes=64)
+            dst = bf[:].rearrange("p (c i) j -> p c j i", i=4)
+            src = wa_raw[i, z][:].rearrange("p j (c i) -> p c j i", i=4)
+            if on_vector:
+                nc.vector.tensor_copy(out=dst, in_=src)
+            else:
+                nc.scalar.copy(out=dst, in_=src)
+            wa_bf[i, z] = bf
+
+        def quantise_wa(i, z):
+            codes = sb.tile([P, P], U32, name="wa_codes_%d_%d" % (i, z), align_bytes=64)
+            plane = sb.tile([P, P], U8, name="wa_plane_%d_%d" % (i, z), align_bytes=64)
+            nc.vector.quantize_mx(
+                out=codes[:].bitcast(FP8X4), scales=plane[:], in_=wa_bf[i, z][:].rearrange("p c j -> p (c j)")
+            )
+            wa_codes[i, z], wa_plane[i, z] = codes, plane
+
+        wq_plane = new_plane("wq_plane")
+        xa_plane = new_plane("xa_plane")
+        wc_plane = new_plane("wc_plane")
+        xq_plane = new_plane("xq_plane")
+
+        xa = load_words("xa", xa_rows)
+        load_wa_pass(0, 0)
+        load_plane(nc.sync, xa_plane, xa_scales, range(4))
+        load_plane(nc.gpsimd, wq_plane, wq_scales, range(4))
+        load_wa_pass(0, 1)
+        wc = load_words("wc", wc_rows)
+        load_plane(nc.sync, wc_plane, wc_scales, range(4))
+        xq = load_words("xq", xq_rows)
+        wq = {}
+        wq[0] = load_words("wq0", wq_rows[:, :, 0:512])[:]
+        load_plane(nc.sync, xq_plane, xq_scales, range(4))
+        load_wa(1)
+        wq_mid = load_words("wq12", wq_rows[:, :, 512:1536])
+        wq[1], wq[2] = wq_mid[:, :, 0:512], wq_mid[:, :, 512:1024]
+        load_wa(2)
+        load_wa(3)
+        wq[3] = load_words("wq3", wq_rows[:, :, 1536:2048])[:]
+
+        p_acc = [ps.tile([P, T], F32, name="p_acc_%d" % i) for i in range(TILES)]
+        r_acc = [ps.tile([P, T], F32, name="r_acc_%d" % i) for i in range(TILES)]
+        r_neg = [sb.tile([P, T], F32, name="r_neg_%d" % i) for i in range(TILES)]
+
+        def mm_r(i):
+            for z in range(PASSES):
+                nc.tensor.matmul_mx(
+                    out=r_acc[i][:],
+                    lhsT=wc[:, z, 2 * P * i : 2 * P * (i + 1)].bitcast(FP4X4),
+                    lhsT_scale=wc_plane[:, z, P * i : P * (i + 1)],
+                    rhs=xa[:, z, :].bitcast(FP8X4),
+                    rhs_scale=xa_plane[:, z, :],
+                    start=(z == 0),
+                    stop=(z == PASSES - 1),
+                )
+
+        def mm_a(i, z, start, stop):
+            nc.tensor.matmul_mx(
+                out=p_acc[i][:],
+                lhsT=wa_codes[i, z][:].bitcast(FP8X4),
+                lhsT_scale=wa_plane[i, z][:],
+                rhs=xa[:, z, :].bitcast(FP8X4),
+                rhs_scale=xa_plane[:, z, :],
+                start=start,
+                stop=stop,
+            )
+
+        def mm_q(i, z, start, stop):
+            nc.tensor.matmul_mx(
+                out=p_acc[i][:],
+                lhsT=wq[i][:, z, :].bitcast(FP8X4),
+                lhsT_scale=wq_plane[:, z, P * i : P * (i + 1)],
+                rhs=xq[:, z, :].bitcast(FP4X4),
+                rhs_scale=xq_plane[:, z, :],
+                start=start,
+                stop=stop,
+            )
+
+        def copy_r(i):
+            nc.scalar.activation(out=r_neg[i][:], in_=r_acc[i][:], func=ACT.Copy, scale=-0.25)
+
+        def finish(i, h):
+            cols = slice(HALF * h, HALF * (h + 1))
+            larger = sb.tile([P, HALF], F32, name="larger_%d_%d" % (i, h))
+            less_p = sb.tile([P, HALF], F32, name="less_p_%d_%d" % (i, h))
+            y = sb.tile([P, HALF], F32, name="y_%d_%d" % (i, h))
+            nc.vector.scalar_tensor_tensor(
+                out=larger[:], in0=r_neg[i][:, cols], scalar=-5.6, in1=p_acc[i][:, cols], op0=ALU.mult, op1=ALU.max
+            )
+            nc.vector.scalar_tensor_tensor(
+                out=less_p[:], in0=p_acc[i][:, cols], scalar=-0.25, in1=larger[:], op0=ALU.mult, op1=ALU.add
+            )
+            if i == TILES - 1 and h == 1:
+                nc.vector.scalar_tensor_tensor(
+                    out=y[:], in0=r_acc[i][:, cols], scalar=-0.25, in1=less_p[:], op0=ALU.mult, op1=ALU.add
+                )
+            else:
+                nc.gpsimd.tensor_tensor(out=y[:], in0=less_p[:], in1=r_neg[i][:, cols], op=ALU.add)
+            nc.sync.dma_start(out=out[P * i : P * (i + 1), cols], in_=y[:])
+
+        for z in range(PASSES):
+            cast_wa(0, z, True)
+            quantise_wa(0, z)
+        mm_a(0, 0, True, False)
+        mm_a(0, 1, False, False)
+        mm_r(0)
+        copy_r(0)
+        mm_q(0, 0, False, False)
+        mm_q(0, 1, False, True)
+        mm_r(1)
+        mm_r(2)
+        cast_wa(1, 0, True)
+        cast_wa(1, 1, False)
+        copy_r(1)
+        quantise_wa(1, 0)
+        finish(0, 0)
+        quantise_wa(1, 1)
+        finish(0, 1)
+        mm_q(1, 0, True, False)
+        mm_q(1, 1, False, False)
+        mm_a(1, 0, False, False)
+        mm_a(1, 1, False, True)
+        mm_r(3)
+        cast_wa(2, 0, False)
+        cast_wa(2, 1, False)
+        copy_r(2)
+        finish(1, 0)
+        quantise_wa(2, 0)
+        finish(1, 1)
+        quantise_wa(2, 1)
+        mm_q(2, 0, True, False)
+        mm_q(2, 1, False, False)
+        mm_a(2, 0, False, False)
+        mm_a(2, 1, False, True)
+        cast_wa(3, 0, False)
+        copy_r(3)
+        cast_wa(3, 1, True)
+        finish(2, 0)
+        quantise_wa(3, 0)
+        quantise_wa(3, 1)
+        finish(2, 1)
+        mm_a(3, 0, True, False)
+        mm_q(3, 0, False, False)
+        mm_q(3, 1, False, False)
+        mm_a(3, 1, False, True)
+        finish(3, 0)
+        finish(3, 1)

@@ -17,9 +17,14 @@ ACT = mybir.ActivationFunctionType
 
 P = 128
 PACK = 4
-PASSES = 2
+FP4_BYTES = 2
+PASSES = K // (P * PACK)
+QUADRANTS = 4
 TILES = N // P
-HALF = T // 2
+LAST = TILES - 1
+PAIRS = ((0, 1), (2, 3))
+LINE = 4
+HALVES = (slice(0, T // 2), slice(T // 2, T))
 
 
 def tile_mix_larger_of_two_sums_kernel(
@@ -32,12 +37,12 @@ def tile_mix_larger_of_two_sums_kernel(
         ctx.enter_context(tc.manual_schedule())
 
         def new_plane(name):
-            plane = sb.tile([P, PASSES, 512], U8, name=name, align_bytes=64)
+            plane = sb.tile([P, PASSES, T], U8, name=name, align_bytes=64)
             nc.vector.memset(plane[:].bitcast(I32), 0)
             return plane
 
-        def load_plane(queue, plane, scales, quads):
-            for q in quads:
+        def load_plane(queue, plane, scales):
+            for q in range(QUADRANTS):
                 queue.dma_start(
                     out=plane[32 * q : 32 * q + 4, :, :].bitcast(I32),
                     in_=scales[:, 4 * q : 4 * q + 4, :].rearrange("z r c -> r z c").bitcast(I32),
@@ -48,168 +53,134 @@ def tile_mix_larger_of_two_sums_kernel(
             nc.sync.dma_start(out=words[:].bitcast(I32), in_=rows.bitcast(I32))
             return words
 
-        xa_rows = xa_words.rearrange("z p c r -> p z (c r)")
-        wq_rows = wq_words.rearrange("z p c r -> p z (c r)")
-        xq_rows = xq_words.rearrange("z p c -> p z c")
-        wc_rows = wc_words.rearrange("z p c -> p z c")
         wa_rows = wa.rearrange("(z p j) n -> z p j n", z=PASSES, j=PACK)
+        wq_rows = wq_words.rearrange("z p c r -> p z (c r)")
+        wa_raw, wa_codes, wa_plane = {}, {}, {}
 
-        wa_raw, wa_bf, wa_codes, wa_plane = {}, {}, {}, {}
+        def load_wa(pair, z):
+            raw = sb.tile([P, PACK, P * len(pair)], F32, name="wa_raw_%d_%d" % (pair[0], z))
+            nc.sync.dma_start(out=raw[:], in_=wa_rows[z, :, :, P * pair[0] : P * (pair[-1] + 1)])
+            wa_raw[pair, z] = raw
 
-        def load_wa_pass(i, z):
-            raw = sb.tile([P, PACK, P], F32, name="wa_raw_%d_%d" % (i, z))
-            nc.sync.dma_start(out=raw[:], in_=wa_rows[z, :, :, P * i : P * (i + 1)])
-            wa_raw[i, z] = raw
-
-        def load_wa(i):
-            for z in range(PASSES):
-                load_wa_pass(i, z)
-
-        def cast_wa(i, z, on_vector):
-            bf = sb.tile([P, P, PACK], BF16, name="wa_bf_%d_%d" % (i, z), align_bytes=64)
-            dst = bf[:].rearrange("p (c i) j -> p c j i", i=4)
-            src = wa_raw[i, z][:].rearrange("p j (c i) -> p c j i", i=4)
-            if on_vector:
-                nc.vector.tensor_copy(out=dst, in_=src)
-            else:
-                nc.scalar.copy(out=dst, in_=src)
-            wa_bf[i, z] = bf
-
-        def quantise_wa(i, z):
-            codes = sb.tile([P, P], U32, name="wa_codes_%d_%d" % (i, z), align_bytes=64)
-            plane = sb.tile([P, P], U8, name="wa_plane_%d_%d" % (i, z), align_bytes=64)
-            nc.vector.quantize_mx(
-                out=codes[:].bitcast(FP8X4), scales=plane[:], in_=wa_bf[i, z][:].rearrange("p c j -> p (c j)")
+        def quantise_wa(pair, z):
+            width = P * len(pair)
+            rounded = sb.tile([P, width, PACK], BF16, name="wa_bf_%d_%d" % (pair[0], z), align_bytes=64)
+            nc.vector.tensor_copy(
+                out=rounded[:].rearrange("p (c e) j -> p c j e", e=LINE),
+                in_=wa_raw[pair, z][:].rearrange("p j (c e) -> p c j e", e=LINE),
             )
-            wa_codes[i, z], wa_plane[i, z] = codes, plane
+            codes = sb.tile([P, width], U32, name="wa_codes_%d_%d" % (pair[0], z), align_bytes=64)
+            plane = sb.tile([P, width], U8, name="wa_plane_%d_%d" % (pair[0], z), align_bytes=64)
+            nc.vector.quantize_mx(
+                out=codes[:].bitcast(FP8X4), scales=plane[:], in_=rounded[:].rearrange("p c j -> p (c j)")
+            )
+            for s, i in enumerate(pair):
+                wa_codes[i, z] = codes[:, P * s : P * (s + 1)]
+                wa_plane[i, z] = plane[:, P * s : P * (s + 1)]
 
         wq_plane = new_plane("wq_plane")
         xa_plane = new_plane("xa_plane")
         wc_plane = new_plane("wc_plane")
         xq_plane = new_plane("xq_plane")
 
-        xa = load_words("xa", xa_rows)
-        load_wa_pass(0, 0)
-        load_plane(nc.sync, xa_plane, xa_scales, range(4))
-        load_plane(nc.gpsimd, wq_plane, wq_scales, range(4))
-        load_wa_pass(0, 1)
-        wc = load_words("wc", wc_rows)
-        load_plane(nc.sync, wc_plane, wc_scales, range(4))
-        xq = load_words("xq", xq_rows)
-        wq = {}
-        wq[0] = load_words("wq0", wq_rows[:, :, 0:512])[:]
-        load_plane(nc.sync, xq_plane, xq_scales, range(4))
-        load_wa(1)
-        wq_mid = load_words("wq12", wq_rows[:, :, 512:1536])
-        wq[1], wq[2] = wq_mid[:, :, 0:512], wq_mid[:, :, 512:1024]
-        load_wa(2)
-        load_wa(3)
-        wq[3] = load_words("wq3", wq_rows[:, :, 1536:2048])[:]
+        load_plane(nc.gpsimd, wq_plane, wq_scales)
+        load_wa(PAIRS[0], 0)
+        xa = load_words("xa", xa_words.rearrange("z p c r -> p z (c r)"))
+        load_plane(nc.sync, xa_plane, xa_scales)
+        load_wa(PAIRS[0], 1)
+        wc = load_words("wc", wc_words.rearrange("z p c -> p z c"))
+        load_wa(PAIRS[1], 0)
+        xq = load_words("xq", xq_words.rearrange("z p c -> p z c"))
+        load_plane(nc.sync, wc_plane, wc_scales)
+        load_wa(PAIRS[1], 1)
+        wq_first = load_words("wq_first", wq_rows[:, :, : PACK * P])
+        load_plane(nc.sync, xq_plane, xq_scales)
+        wq_rest = load_words("wq_rest", wq_rows[:, :, PACK * P :])
+        wq = [wq_first[:]] + [wq_rest[:, :, PACK * P * s : PACK * P * (s + 1)] for s in range(LAST)]
 
         p_acc = [ps.tile([P, T], F32, name="p_acc_%d" % i) for i in range(TILES)]
         r_acc = [ps.tile([P, T], F32, name="r_acc_%d" % i) for i in range(TILES)]
         r_neg = [sb.tile([P, T], F32, name="r_neg_%d" % i) for i in range(TILES)]
+        larger = [sb.tile([P, T], F32, name="larger_%d" % i) for i in range(TILES)]
+        less_p = [sb.tile([P, T], F32, name="less_p_%d" % i) for i in range(TILES)]
+        y = [sb.tile([P, T], F32, name="y_%d" % i) for i in range(TILES)]
 
-        def mm_r(i):
+        def product_wc(i):
             for z in range(PASSES):
                 nc.tensor.matmul_mx(
                     out=r_acc[i][:],
-                    lhsT=wc[:, z, 2 * P * i : 2 * P * (i + 1)].bitcast(FP4X4),
+                    lhsT=wc[:, z, FP4_BYTES * P * i : FP4_BYTES * P * (i + 1)].bitcast(FP4X4),
                     lhsT_scale=wc_plane[:, z, P * i : P * (i + 1)],
                     rhs=xa[:, z, :].bitcast(FP8X4),
                     rhs_scale=xa_plane[:, z, :],
                     start=(z == 0),
                     stop=(z == PASSES - 1),
                 )
-
-        def mm_a(i, z, start, stop):
-            nc.tensor.matmul_mx(
-                out=p_acc[i][:],
-                lhsT=wa_codes[i, z][:].bitcast(FP8X4),
-                lhsT_scale=wa_plane[i, z][:],
-                rhs=xa[:, z, :].bitcast(FP8X4),
-                rhs_scale=xa_plane[:, z, :],
-                start=start,
-                stop=stop,
-            )
-
-        def mm_q(i, z, start, stop):
-            nc.tensor.matmul_mx(
-                out=p_acc[i][:],
-                lhsT=wq[i][:, z, :].bitcast(FP8X4),
-                lhsT_scale=wq_plane[:, z, P * i : P * (i + 1)],
-                rhs=xq[:, z, :].bitcast(FP4X4),
-                rhs_scale=xq_plane[:, z, :],
-                start=start,
-                stop=stop,
-            )
-
-        def copy_r(i):
             nc.scalar.activation(out=r_neg[i][:], in_=r_acc[i][:], func=ACT.Copy, scale=-0.25)
 
-        def finish(i, h):
-            cols = slice(HALF * h, HALF * (h + 1))
-            larger = sb.tile([P, HALF], F32, name="larger_%d_%d" % (i, h))
-            less_p = sb.tile([P, HALF], F32, name="less_p_%d_%d" % (i, h))
-            y = sb.tile([P, HALF], F32, name="y_%d_%d" % (i, h))
-            nc.vector.scalar_tensor_tensor(
-                out=larger[:], in0=r_neg[i][:, cols], scalar=-5.6, in1=p_acc[i][:, cols], op0=ALU.mult, op1=ALU.max
+        def pass_wa(i, z):
+            nc.tensor.matmul_mx(
+                out=p_acc[i][:],
+                lhsT=wa_codes[i, z].bitcast(FP8X4),
+                lhsT_scale=wa_plane[i, z],
+                rhs=xa[:, z, :].bitcast(FP8X4),
+                rhs_scale=xa_plane[:, z, :],
+                start=(z == 0),
+                stop=False,
             )
-            nc.vector.scalar_tensor_tensor(
-                out=less_p[:], in0=p_acc[i][:, cols], scalar=-0.25, in1=larger[:], op0=ALU.mult, op1=ALU.add
-            )
-            if i == TILES - 1 and h == 1:
-                nc.vector.scalar_tensor_tensor(
-                    out=y[:], in0=r_acc[i][:, cols], scalar=-0.25, in1=less_p[:], op0=ALU.mult, op1=ALU.add
+
+        def product_wq(i):
+            for z in range(PASSES):
+                nc.tensor.matmul_mx(
+                    out=p_acc[i][:],
+                    lhsT=wq[i][:, z, :].bitcast(FP8X4),
+                    lhsT_scale=wq_plane[:, z, P * i : P * (i + 1)],
+                    rhs=xq[:, z, :].bitcast(FP4X4),
+                    rhs_scale=xq_plane[:, z, :],
+                    start=False,
+                    stop=(z == PASSES - 1),
                 )
+
+        def take_larger(i, cols):
+            nc.vector.scalar_tensor_tensor(
+                out=larger[i][:, cols], in0=r_neg[i][:, cols], scalar=-5.6, in1=p_acc[i][:, cols],
+                op0=ALU.mult, op1=ALU.max,
+            )
+
+        def subtract_p(i, cols):
+            nc.vector.scalar_tensor_tensor(
+                out=less_p[i][:, cols], in0=p_acc[i][:, cols], scalar=-0.25, in1=larger[i][:, cols],
+                op0=ALU.mult, op1=ALU.add,
+            )
+
+        def subtract_r_and_store(i, cols):
+            if i < LAST:
+                nc.gpsimd.tensor_tensor(out=y[i][:, cols], in0=less_p[i][:, cols], in1=r_neg[i][:, cols], op=ALU.add)
+                nc.sync.dma_start(out=out[P * i : P * (i + 1), cols], in_=y[i][:, cols])
             else:
-                nc.gpsimd.tensor_tensor(out=y[:], in0=less_p[:], in1=r_neg[i][:, cols], op=ALU.add)
-            nc.sync.dma_start(out=out[P * i : P * (i + 1), cols], in_=y[:])
+                nc.vector.scalar_tensor_tensor(
+                    out=y[i][:, cols], in0=r_acc[i][:, cols], scalar=-0.25, in1=less_p[i][:, cols],
+                    op0=ALU.mult, op1=ALU.add,
+                )
+                nc.scalar.dma_start(out=out[P * i : P * (i + 1), cols], in_=y[i][:, cols])
 
         for z in range(PASSES):
-            cast_wa(0, z, True)
-            quantise_wa(0, z)
-        mm_a(0, 0, True, False)
-        mm_a(0, 1, False, False)
-        mm_r(0)
-        copy_r(0)
-        mm_q(0, 0, False, False)
-        mm_q(0, 1, False, True)
-        mm_r(1)
-        mm_r(2)
-        cast_wa(1, 0, True)
-        cast_wa(1, 1, False)
-        copy_r(1)
-        quantise_wa(1, 0)
-        finish(0, 0)
-        quantise_wa(1, 1)
-        finish(0, 1)
-        mm_q(1, 0, True, False)
-        mm_q(1, 1, False, False)
-        mm_a(1, 0, False, False)
-        mm_a(1, 1, False, True)
-        mm_r(3)
-        cast_wa(2, 0, False)
-        cast_wa(2, 1, False)
-        copy_r(2)
-        finish(1, 0)
-        quantise_wa(2, 0)
-        finish(1, 1)
-        quantise_wa(2, 1)
-        mm_q(2, 0, True, False)
-        mm_q(2, 1, False, False)
-        mm_a(2, 0, False, False)
-        mm_a(2, 1, False, True)
-        cast_wa(3, 0, False)
-        copy_r(3)
-        cast_wa(3, 1, True)
-        finish(2, 0)
-        quantise_wa(3, 0)
-        quantise_wa(3, 1)
-        finish(2, 1)
-        mm_a(3, 0, True, False)
-        mm_q(3, 0, False, False)
-        mm_q(3, 1, False, False)
-        mm_a(3, 1, False, True)
-        finish(3, 0)
-        finish(3, 1)
+            quantise_wa(PAIRS[0], z)
+            for i in PAIRS[0]:
+                pass_wa(i, z)
+        for i in range(LAST):
+            product_wc(i)
+        for z in range(PASSES):
+            quantise_wa(PAIRS[1], z)
+        product_wq(0)
+        product_wc(LAST)
+        product_wq(1)
+        for i in PAIRS[1]:
+            for z in range(PASSES):
+                pass_wa(i, z)
+            product_wq(i)
+
+        for i in range(TILES):
+            for step in (take_larger, subtract_p, subtract_r_and_store):
+                for cols in HALVES:
+                    step(i, cols)

from contextlib import ExitStack

import concourse.mybir as mybir

K, L, T, N = 1024, 1024, 512, 512
FLOPS = 2 * N * T * (K + L + K)

F32 = mybir.dt.float32
BF16 = mybir.dt.bfloat16
I32 = mybir.dt.int32
U32 = mybir.dt.uint32
U8 = mybir.dt.uint8
FP8X4 = mybir.dt.float8_e4m3fn_x4
FP4X4 = mybir.dt.float4_e2m1fn_x4
ALU = mybir.AluOpType
ACT = mybir.ActivationFunctionType

P = 128
PACK = 4
FP4_BYTES = 2
PASSES = K // (P * PACK)
QUADRANTS = 4
TILES = N // P
LAST = TILES - 1
PAIRS = ((0, 1), (2, 3))
LINE = 4
HALVES = (slice(0, T // 2), slice(T // 2, T))


def tile_mix_larger_of_two_sums_kernel(
    tc, xa_words, xa_scales, wa, xq_words, xq_scales, wq_words, wq_scales, wc_words, wc_scales, out
):
    nc = tc.nc
    with ExitStack() as ctx:
        sb = ctx.enter_context(tc.tile_pool(name="sb", bufs=1))
        ps = ctx.enter_context(tc.psum_pool(name="ps", bufs=1))
        ctx.enter_context(tc.manual_schedule())

        def new_plane(name):
            plane = sb.tile([P, PASSES, T], U8, name=name, align_bytes=64)
            nc.vector.memset(plane[:].bitcast(I32), 0)
            return plane

        def load_plane(queue, plane, scales):
            for q in range(QUADRANTS):
                queue.dma_start(
                    out=plane[32 * q : 32 * q + 4, :, :].bitcast(I32),
                    in_=scales[:, 4 * q : 4 * q + 4, :].rearrange("z r c -> r z c").bitcast(I32),
                )

        def load_words(name, rows):
            words = sb.tile([P, PASSES, rows.shape[2]], U8, name=name, align_bytes=64)
            nc.sync.dma_start(out=words[:].bitcast(I32), in_=rows.bitcast(I32))
            return words

        wa_rows = wa.rearrange("(z p j) n -> z p j n", z=PASSES, j=PACK)
        wq_rows = wq_words.rearrange("z p c r -> p z (c r)")
        wa_raw, wa_codes, wa_plane = {}, {}, {}

        def load_wa(pair, z):
            raw = sb.tile([P, PACK, P * len(pair)], F32, name="wa_raw_%d_%d" % (pair[0], z))
            nc.sync.dma_start(out=raw[:], in_=wa_rows[z, :, :, P * pair[0] : P * (pair[-1] + 1)])
            wa_raw[pair, z] = raw

        def quantise_wa(pair, z):
            width = P * len(pair)
            rounded = sb.tile([P, width, PACK], BF16, name="wa_bf_%d_%d" % (pair[0], z), align_bytes=64)
            nc.vector.tensor_copy(
                out=rounded[:].rearrange("p (c e) j -> p c j e", e=LINE),
                in_=wa_raw[pair, z][:].rearrange("p j (c e) -> p c j e", e=LINE),
            )
            codes = sb.tile([P, width], U32, name="wa_codes_%d_%d" % (pair[0], z), align_bytes=64)
            plane = sb.tile([P, width], U8, name="wa_plane_%d_%d" % (pair[0], z), align_bytes=64)
            nc.vector.quantize_mx(
                out=codes[:].bitcast(FP8X4), scales=plane[:], in_=rounded[:].rearrange("p c j -> p (c j)")
            )
            for s, i in enumerate(pair):
                wa_codes[i, z] = codes[:, P * s : P * (s + 1)]
                wa_plane[i, z] = plane[:, P * s : P * (s + 1)]

        wq_plane = new_plane("wq_plane")
        xa_plane = new_plane("xa_plane")
        wc_plane = new_plane("wc_plane")
        xq_plane = new_plane("xq_plane")

        load_plane(nc.gpsimd, wq_plane, wq_scales)
        load_wa(PAIRS[0], 0)
        xa = load_words("xa", xa_words.rearrange("z p c r -> p z (c r)"))
        load_plane(nc.sync, xa_plane, xa_scales)
        load_wa(PAIRS[0], 1)
        wc = load_words("wc", wc_words.rearrange("z p c -> p z c"))
        load_wa(PAIRS[1], 0)
        xq = load_words("xq", xq_words.rearrange("z p c -> p z c"))
        load_plane(nc.sync, wc_plane, wc_scales)
        load_wa(PAIRS[1], 1)
        wq_first = load_words("wq_first", wq_rows[:, :, : PACK * P])
        load_plane(nc.sync, xq_plane, xq_scales)
        wq_rest = load_words("wq_rest", wq_rows[:, :, PACK * P :])
        wq = [wq_first[:]] + [wq_rest[:, :, PACK * P * s : PACK * P * (s + 1)] for s in range(LAST)]

        p_acc = [ps.tile([P, T], F32, name="p_acc_%d" % i) for i in range(TILES)]
        r_acc = [ps.tile([P, T], F32, name="r_acc_%d" % i) for i in range(TILES)]
        r_neg = [sb.tile([P, T], F32, name="r_neg_%d" % i) for i in range(TILES)]
        larger = [sb.tile([P, T], F32, name="larger_%d" % i) for i in range(TILES)]
        less_p = [sb.tile([P, T], F32, name="less_p_%d" % i) for i in range(TILES)]
        y = [sb.tile([P, T], F32, name="y_%d" % i) for i in range(TILES)]

        def product_wc(i):
            for z in range(PASSES):
                nc.tensor.matmul_mx(
                    out=r_acc[i][:],
                    lhsT=wc[:, z, FP4_BYTES * P * i : FP4_BYTES * P * (i + 1)].bitcast(FP4X4),
                    lhsT_scale=wc_plane[:, z, P * i : P * (i + 1)],
                    rhs=xa[:, z, :].bitcast(FP8X4),
                    rhs_scale=xa_plane[:, z, :],
                    start=(z == 0),
                    stop=(z == PASSES - 1),
                )
            nc.scalar.activation(out=r_neg[i][:], in_=r_acc[i][:], func=ACT.Copy, scale=-0.25)

        def pass_wa(i, z):
            nc.tensor.matmul_mx(
                out=p_acc[i][:],
                lhsT=wa_codes[i, z].bitcast(FP8X4),
                lhsT_scale=wa_plane[i, z],
                rhs=xa[:, z, :].bitcast(FP8X4),
                rhs_scale=xa_plane[:, z, :],
                start=(z == 0),
                stop=False,
            )

        def product_wq(i):
            for z in range(PASSES):
                nc.tensor.matmul_mx(
                    out=p_acc[i][:],
                    lhsT=wq[i][:, z, :].bitcast(FP8X4),
                    lhsT_scale=wq_plane[:, z, P * i : P * (i + 1)],
                    rhs=xq[:, z, :].bitcast(FP4X4),
                    rhs_scale=xq_plane[:, z, :],
                    start=False,
                    stop=(z == PASSES - 1),
                )

        def take_larger(i, cols):
            nc.vector.scalar_tensor_tensor(
                out=larger[i][:, cols], in0=r_neg[i][:, cols], scalar=-5.6, in1=p_acc[i][:, cols],
                op0=ALU.mult, op1=ALU.max,
            )

        def subtract_p(i, cols):
            nc.vector.scalar_tensor_tensor(
                out=less_p[i][:, cols], in0=p_acc[i][:, cols], scalar=-0.25, in1=larger[i][:, cols],
                op0=ALU.mult, op1=ALU.add,
            )

        def subtract_r_and_store(i, cols):
            if i < LAST:
                nc.gpsimd.tensor_tensor(out=y[i][:, cols], in0=less_p[i][:, cols], in1=r_neg[i][:, cols], op=ALU.add)
                nc.sync.dma_start(out=out[P * i : P * (i + 1), cols], in_=y[i][:, cols])
            else:
                nc.vector.scalar_tensor_tensor(
                    out=y[i][:, cols], in0=r_acc[i][:, cols], scalar=-0.25, in1=less_p[i][:, cols],
                    op0=ALU.mult, op1=ALU.add,
                )
                nc.scalar.dma_start(out=out[P * i : P * (i + 1), cols], in_=y[i][:, cols])

        for z in range(PASSES):
            quantise_wa(PAIRS[0], z)
            for i in PAIRS[0]:
                pass_wa(i, z)
        for i in range(LAST):
            product_wc(i)
        for z in range(PASSES):
            quantise_wa(PAIRS[1], z)
        product_wq(0)
        product_wc(LAST)
        product_wq(1)
        for i in PAIRS[1]:
            for z in range(PASSES):
                pass_wa(i, z)
            product_wq(i)

        for i in range(TILES):
            for step in (take_larger, subtract_p, subtract_r_and_store):
                for cols in HALVES:
                    step(i, cols)
